import numpy as np
import ml_dtypes


def mxq(x, axis, fmt="e4m3"):
    dtype, down = {"e4m3": (ml_dtypes.float8_e4m3fn, 7), "e5m2": (ml_dtypes.float8_e5m2, 14)}[fmt]
    v = np.moveaxis(np.asarray(x, np.float32).astype(ml_dtypes.bfloat16).astype(np.float64), axis, -1)
    blocks = v.reshape(v.shape[:-1] + (-1, 32))
    amax = np.abs(blocks).max(-1, keepdims=True)
    byte = np.maximum(np.where(amax > 0, np.frexp(amax)[1] - 1 + 127, 0) - down, 1)
    scale = np.exp2(byte - 127.0)
    codes = (blocks / scale).astype(np.float32).astype(dtype).astype(np.float64)
    return np.moveaxis((codes * scale).reshape(v.shape), -1, axis)


WIDE = False


def mx_kscale(k):
    if not WIDE:
        return np.ones(k)
    levels = np.array([10, -10, 5, -5, 0])
    if k % 512:
        return np.exp2(np.random.permutation(np.resize(levels, k // 32))).repeat(32)
    a = np.empty((k // 512, 16))
    for p in range(k // 512):
        a[p, :8] = np.random.permutation(np.resize(levels, 8))
        for g in range(8):
            far = levels[np.abs(levels - a[p, g]) >= 10]
            a[p, g + 8] = far[np.random.randint(len(far))]
    return np.exp2(a.ravel()).repeat(32)


def f64(x):
    return np.asarray(x).astype(np.float64)


def striped(idx):
    return np.tile(idx.reshape(-1, 16).T, (8, 1)).astype(np.uint16)


def unstriped(offs):
    return offs[:16].T.reshape(-1).astype(np.int64)


def silu(v):
    return v / (1.0 + np.exp(-np.maximum(v, -700.0)))


K, T, E, C, H, N = 1536, 768, 6, 256, 512, 128


def by_expert(wq, xq):
    return np.concatenate([wq[e].T @ xq[:, e * C:(e + 1) * C] for e in range(E)], axis=1)


def setup_inputs():
    n = np.random.standard_normal
    s = mx_kscale(K)[:, None]
    u = mx_kscale(H)
    first = np.random.permutation(np.repeat(np.arange(E), T // E))
    second = (first + 1 + np.random.permutation(np.repeat(np.arange(E - 1), -(-T // (E - 1)))[:T])) % E
    while np.bincount(second, minlength=E).max() != T // E:
        load = np.bincount(second, minlength=E); hi, lo = int(load.argmax()), int(load.argmin())
        t = np.flatnonzero((second == hi) & (first != lo))[0]; second[t] = lo
    slot_token = np.empty(E * C, np.int64); pos = np.empty((2, T), np.int64); fill = np.zeros(E, np.int64)
    place = np.stack([np.random.permutation(C) for _ in range(E)])
    for r, deal in enumerate((first, second)):
        for t in np.random.permutation(T):
            e = deal[t]; j = e * C + place[e, fill[e]]; fill[e] += 1; slot_token[j] = t; pos[r, t] = j
    g = np.random.uniform(0.2, 0.8, T)
    return {
        "xT": (n((K, T)) * s).astype(np.float32),
        "w1": (n((E, K, H)) / np.sqrt(K) / s[None] * u[None, None, :]).astype(np.float32),
        "w2": (n((E, H, N)) / np.sqrt(H) / u[None, :, None]).astype(np.float32),
        "gate": np.stack([np.tile(g, (N, 1)), np.tile(1.0 - g, (N, 1))]).astype(np.float32),
        "offs": striped(slot_token),
        "pos1": striped(pos[0]),
        "pos2": striped(pos[1]),
    }


def reference(xT, w1, w2, gate, offs, pos1, pos2):
    idx = unstriped(offs)
    xq = mxq(f64(xT)[:, idx], 0, "e4m3")
    h = silu(by_expert(mxq(f64(w1), 1, "e4m3"), xq))
    y = by_expert(mxq(f64(w2), 1, "e4m3"), mxq(h, 0, "e4m3"))
    return f64(gate[0]) * y[:, unstriped(pos1)] + f64(gate[1]) * y[:, unstriped(pos2)]

@@ -1,0 +1,317 @@
+from contextlib import ExitStack
+
+import concourse.mybir as mybir
+
+K, T, E, C, H, N = 1536, 768, 6, 256, 512, 128
+FLOPS = 2 * E * C * (K * H + H * N)
+
+F32 = mybir.dt.float32
+BF16 = mybir.dt.bfloat16
+U32 = mybir.dt.uint32
+U16 = mybir.dt.uint16
+U8 = mybir.dt.uint8
+FP8X4 = mybir.dt.float8_e4m3fn_x4
+SILU = mybir.ActivationFunctionType.Silu
+MULT = mybir.AluOpType.mult
+ADD = mybir.AluOpType.add
+
+P = 128
+PACK = 4
+K_PASS = P * PACK
+PASSES = K // K_PASS
+SLICE = 2 * C
+SLICES = E * C // SLICE
+HALF = C // 2
+
+X_SPLIT = 512
+AHEAD = 7
+
+
+def tile_routed_moe_kernel(tc, xT, w1, w2, gate, offs, pos1, pos2, out):
+    nc = tc.nc
+    with ExitStack() as ctx:
+        keep = ctx.enter_context(tc.tile_pool(name="keep", bufs=1))
+        xraw_pool = ctx.enter_context(tc.tile_pool(name="xraw_pool", bufs=3))
+        wraw_pool = ctx.enter_context(tc.tile_pool(name="wraw_pool", bufs=AHEAD + 1))
+        bf_pool = ctx.enter_context(tc.tile_pool(name="bf_pool", bufs=4))
+        xbf_pool = ctx.enter_context(tc.tile_pool(name="xbf_pool", bufs=2))
+        code_pool = ctx.enter_context(tc.tile_pool(name="code_pool", bufs=6))
+        h_pool = ctx.enter_context(tc.tile_pool(name="h_pool", bufs=2))
+        psum = ctx.enter_context(tc.psum_pool(name="psum", bufs=2))
+        last_psum = ctx.enter_context(tc.psum_pool(name="last_psum", bufs=1))
+
+        offs_t = keep.tile([P, E * C // 16], U16, name="offs_t")
+        pos_t = [keep.tile([P, T // 16], U16, name=f"pos_t{r}") for r in range(2)]
+        gate_t = keep.tile([P, 2, T], F32, name="gate_t")
+        y_all = keep.tile([P, E * C], F32, name="y_all")
+        tok_words = [keep.tile([P, T], U32, name=f"tok_words{g}", align_bytes=64) for g in range(PASSES)]
+        tok_bytes = keep.tile([P, T], U8, name="tok_bytes", align_bytes=64)
+        slot_words = [[keep.tile([P, SLICE], U32, name=f"slot_words{s}_{g}", align_bytes=64) for g in range(PASSES)] for s in range(SLICES)]
+        slot_bytes = [keep.tile([P, SLICE], U8, name=f"slot_bytes{s}", align_bytes=64) for s in range(SLICES)]
+        w2_raw = keep.tile([P, E, PACK, N], F32, name="w2_raw")
+        w2_bf = keep.tile([P, E * N * PACK], BF16, name="w2_bf", align_bytes=64)
+        w2_codes = keep.tile([P, E * N], U32, name="w2_codes", align_bytes=64)
+        w2_scales = keep.tile([P, E * N], U8, name="w2_scales", align_bytes=64)
+        zero = keep.tile([P, 1], F32, name="zero")
+        silu_zero = keep.tile([P, 1], F32, name="silu_zero")
+
+        nc.gpsimd.memset(zero[:], 0.0)
+        nc.scalar.activation(silu_zero[:], zero[:], SILU)
+        nc.gpsimd.memset(tok_bytes[:], 0)
+
+        x_raw = []
+        for g in range(PASSES):
+            x_raw.append(xraw_pool.tile([P, PACK, T], F32, name="x_raw"))
+            src = xT[g * K_PASS : (g + 1) * K_PASS, :].rearrange("(p j) t -> p j t", j=PACK)
+            for cols in (slice(0, X_SPLIT), slice(X_SPLIT, T)) if g == 0 else (slice(0, T),):
+                nc.sync.dma_start(out=x_raw[g][:, :, cols], in_=src[:, :, cols])
+            if g == 0:
+                nc.sync.dma_start(out=offs_t[:], in_=offs)
+
+        chunks = [(e, g) for e in range(E) for g in range(PASSES)]
+        w_raw = {}
+
+        def load_w2(e0, e1):
+            nc.sync.dma_start(out=w2_raw[:, e0:e1], in_=w2[e0:e1].rearrange("e (p j) n -> p e j n", j=PACK))
+
+        def load(i):
+            e, g = chunks[i]
+            w_raw[i] = wraw_pool.tile([P, PACK, H], F32, name="w_raw")
+            src = w1[e, g * K_PASS : (g + 1) * K_PASS, :].rearrange("(p j) h -> p j h", j=PACK)
+            if i < len(chunks) - 1:
+                nc.sync.dma_start(out=w_raw[i][:], in_=src)
+            else:
+                for q in range(2):
+                    cols = slice(q * H // 2, (q + 1) * H // 2)
+                    nc.sync.dma_start(out=w_raw[i][:, :, cols], in_=src[:, :, cols])
+                load_w2(E - 1, E)
+                for r, pos in enumerate((pos1, pos2)):
+                    nc.sync.dma_start(out=pos_t[r][:], in_=pos)
+                nc.sync.dma_start(out=gate_t[:], in_=gate.rearrange("r p t -> p r t"))
+            if i == 4:
+                load_w2(0, 4)
+            if i == 14:
+                load_w2(4, 5)
+
+        for i in range(AHEAD):
+            load(i)
+
+        for g in range(PASSES):
+            x_bf = xbf_pool.tile([P, T * PACK], BF16, name="x_bf", align_bytes=64)
+            dst = x_bf[:].rearrange("p (c i j) -> p c j i", i=4, j=PACK)
+            src = x_raw[g][:].rearrange("p j (c i) -> p c j i", i=4)
+            split = X_SPLIT // 4
+            nc.vector.tensor_copy(out=dst[:, :split], in_=src[:, :split])
+            nc.scalar.copy(out=dst[:, split:], in_=src[:, split:])
+            for t0, t1 in ((0, 512), (512, T)):
+                nc.vector.quantize_mx(
+                    out=tok_words[g][:, t0:t1].bitcast(FP8X4),
+                    scales=tok_bytes[4 * g : P, t0:t1],
+                    in_=x_bf[:, PACK * t0 : PACK * t1],
+                )
+
+        def gather_words(s, g):
+            nc.vector.tensor_copy(out=slot_words[s][g][:], in_=tok_words[g][:].indirect(offs_t[:, s * SLICE // 16 : (s + 1) * SLICE // 16]))
+
+        def gather_bytes(s):
+            nc.vector.tensor_copy(out=slot_bytes[s][:], in_=tok_bytes[:].indirect(offs_t[:, s * SLICE // 16 : (s + 1) * SLICE // 16]))
+
+        w_bf = {}
+        w_codes = {}
+        w_scales = {}
+
+        def interleave(i):
+            w_bf[i] = bf_pool.tile([P, H * PACK], BF16, name="w_bf", align_bytes=64)
+            dst = w_bf[i][:].rearrange("p (t m j) -> p m j t", t=PACK, j=PACK)
+            src = w_raw[i][:].rearrange("p j (m t) -> p m j t", t=PACK)
+            if i % PASSES == 1:
+                nc.vector.tensor_copy(out=dst, in_=src)
+            else:
+                nc.scalar.copy(out=dst, in_=src)
+
+        def interleave_last(i):
+            w_bf[i] = bf_pool.tile([P, H * PACK], BF16, name="w_bf", align_bytes=64)
+            dst = w_bf[i][:].rearrange("p (t m j) -> p m j t", t=PACK, j=PACK)
+            src = w_raw[i][:].rearrange("p j (m t) -> p m j t", t=PACK)
+            for q in range(2):
+                m0 = 64 * q
+                nc.scalar.copy(out=dst[:, m0 : m0 + 24], in_=src[:, m0 : m0 + 24])
+                nc.vector.tensor_copy(out=dst[:, m0 + 24 : m0 + 64], in_=src[:, m0 + 24 : m0 + 64])
+
+        def quantize(i):
+            w_codes[i] = code_pool.tile([P, H], U32, name="w_codes", align_bytes=64)
+            w_scales[i] = code_pool.tile([P, H], U8, name="w_scales", align_bytes=64)
+            nc.vector.quantize_mx(out=w_codes[i][:].bitcast(FP8X4), scales=w_scales[i][:], in_=w_bf[i][:])
+
+        def prepare_w2(e0, e1):
+            dst = w2_bf[:, e0 * N * PACK : e1 * N * PACK].rearrange("p (e c i j) -> p e c j i", c=N // 4, i=4, j=PACK)
+            src = w2_raw[:, e0:e1].rearrange("p e j (c i) -> p e c j i", i=4)
+            if e1 - e0 == 4:
+                nc.scalar.copy(out=dst[:, 0:2], in_=src[:, 0:2])
+                nc.vector.tensor_copy(out=dst[:, 2:4], in_=src[:, 2:4])
+            else:
+                nc.vector.tensor_copy(out=dst[:, 0], in_=src[:, 0])
+
+        def quantize_w2(e0, e1):
+            cols = slice(e0 * N, e1 * N)
+            nc.vector.quantize_mx(
+                out=w2_codes[:, cols].bitcast(FP8X4),
+                scales=w2_scales[:, cols],
+                in_=w2_bf[:, e0 * N * PACK : e1 * N * PACK],
+            )
+
+        def layer1_pass(acc, e, g, t, c0, c1):
+            i = PASSES * e + g
+            s, base = divmod(e * C, SLICE)
+            m_cols = slice(t * P, (t + 1) * P)
+            n_cols = slice(base + c0, base + c1)
+            nc.tensor.matmul_mx(
+                out=acc,
+                lhsT=w_codes[i][:, m_cols].bitcast(FP8X4),
+                lhsT_scale=w_scales[i][:, m_cols],
+                rhs=slot_words[s][g][:, n_cols].bitcast(FP8X4),
+                rhs_scale=slot_bytes[s][4 * g : P, n_cols],
+                start=(g == 0),
+                stop=(g == PASSES - 1),
+            )
+
+        def layer1(e):
+            accs = []
+            for half in range(2):
+                acc = psum.tile([P, PACK, HALF], F32, name="acc")
+                for t in range(PACK):
+                    for g in range(PASSES):
+                        layer1_pass(acc[:, t, :], e, g, t, half * HALF, (half + 1) * HALF)
+                accs.append(acc)
+            return accs
+
+        def silu(accs):
+            h_bf = h_pool.tile([P, C * PACK], BF16, name="h_bf", align_bytes=64)
+            for half in range(2):
+                nc.scalar.activation(
+                    h_bf[:, half * HALF * PACK : (half + 1) * HALF * PACK].rearrange("p (n t) -> p n t", t=PACK),
+                    accs[half][:].rearrange("p t n -> p n t"),
+                    SILU,
+                )
+            return h_bf
+
+        def quantize_h(h_bf):
+            h_codes = h_pool.tile([P, C], U32, name="h_codes", align_bytes=64)
+            h_scales = h_pool.tile([P, C], U8, name="h_scales", align_bytes=64)
+            nc.vector.quantize_mx(out=h_codes[:].bitcast(FP8X4), scales=h_scales[:], in_=h_bf[:])
+            return h_codes, h_scales
+
+        def layer2(y, e, h, c0, c1):
+            h_codes, h_scales = h
+            m_cols = slice(e * N, (e + 1) * N)
+            nc.tensor.matmul_mx(
+                out=y,
+                lhsT=w2_codes[:, m_cols].bitcast(FP8X4),
+                lhsT_scale=w2_scales[:, m_cols],
+                rhs=h_codes[:, c0:c1].bitcast(FP8X4),
+                rhs_scale=h_scales[:, c0:c1],
+                start=True,
+                stop=True,
+            )
+
+        def hidden_codes(e):
+            hq[e] = quantize_h(h_bf[e])
+            if e > 0:
+                for d in (0, 1) if e == 1 else (e,):
+                    y_acc[d] = psum.tile([P, C], F32, name="y")
+                    layer2(y_acc[d][:], d, hq[d], 0, C)
+
+        def y_out(e):
+            if e > 0:
+                for d in (0, 1) if e == 1 else (e,):
+                    nc.scalar.copy(out=y_all[:, d * C : (d + 1) * C], in_=y_acc[d][:])
+
+        for g in range(PASSES):
+            gather_words(0, g)
+        gather_bytes(0)
+
+        pending = []
+        for s in range(1, SLICES):
+            for g in range(PASSES):
+                pending.append((s, g))
+            pending.append((s, PASSES))
+
+        h_bf = {}
+        hq = {}
+        y_acc = {}
+        acc_of = {}
+        last = len(chunks) - 1
+        last_acc = [last_psum.tile([P, C], F32, name=f"last_acc{t}") for t in range(PACK)]
+        for i, (e, g) in enumerate(chunks):
+            if i + AHEAD <= last:
+                load(i + AHEAD)
+            if i < last:
+                interleave(i)
+            else:
+                interleave_last(i)
+            if g == 0 and e > 0:
+                quantize(i - 1)
+                if e > 1:
+                    hidden_codes(e - 2)
+                acc_of[e - 1] = layer1(e - 1)
+            if 1 <= i <= len(pending):
+                s, gg = pending[i - 1]
+                if gg < PASSES:
+                    gather_words(s, gg)
+                else:
+                    gather_bytes(s)
+            if g == 1:
+                quantize(i - 1)
+                quantize(i)
+            if g == 2 and e > 0:
+                y_out(e - 2)
+                h_bf[e - 1] = silu(acc_of[e - 1])
+            if i == 5:
+                prepare_w2(0, 4)
+                quantize_w2(0, 4)
+            if i == 14:
+                prepare_w2(4, 5)
+                quantize_w2(4, 5)
+            if i == last:
+                quantize(i)
+            if e == E - 1 and g > 0:
+                for gg in ((0, 1) if g == 1 else (2,)):
+                    for t in range(PACK):
+                        layer1_pass(last_acc[t][:], e, gg, t, 0, C)
+            if i == last:
+                hidden_codes(E - 2)
+                y_out(E - 2)
+
+        prepare_w2(E - 1, E)
+        quantize_w2(E - 1, E)
+        h_rows = h_pool.tile([P, PACK, C], BF16, name="h_rows")
+        for t in range(PACK):
+            nc.scalar.activation(h_rows[:, t, :], last_acc[t][:], SILU)
+        h_last = h_pool.tile([P, C * PACK], BF16, name="h_bf", align_bytes=64)
+        nc.vector.tensor_copy(
+            out=h_last[:].rearrange("p (c i t) -> p c t i", i=4, t=PACK),
+            in_=h_rows[:].rearrange("p t (c i) -> p c t i", i=4),
+        )
+        h = quantize_h(h_last)
+        for half in range(2):
+            y = psum.tile([P, C], F32, name="y")
+            layer2(y[:, :HALF], E - 1, h, half * HALF, (half + 1) * HALF)
+            dst = y_all[:, (E - 1) * C + half * HALF : (E - 1) * C + (half + 1) * HALF]
+            if half == 0:
+                nc.vector.tensor_copy(out=dst, in_=y[:, :HALF])
+            else:
+                nc.scalar.copy(out=dst, in_=y[:, :HALF])
+
+        for t0, t1 in ((0, 512), (512, T)):
+            cols = slice(t0, t1)
+            part = [h_pool.tile([P, 512], F32, name=f"part{r}") for r in range(2)]
+            for r in range(2):
+                nc.vector.tensor_tensor(
+                    part[r][:, : t1 - t0],
+                    y_all[:].indirect(pos_t[r][:, t0 // 16 : t1 // 16]),
+                    gate_t[:, r, cols],
+                    MULT,
+                )
+            total = h_pool.tile([P, 512], F32, name="total")
+            nc.vector.tensor_tensor(total[:, : t1 - t0], part[0][:, : t1 - t0], part[1][:, : t1 - t0], ADD)
+            nc.sync.dma_start(out=out[:, cols], in_=total[:, : t1 - t0])

@@ -19,26 +19,30 @@ P = 128
 PACK = 4
 K_PASS = P * PACK
 PASSES = K // K_PASS
-SLICE = 2 * C
-SLICES = E * C // SLICE
 HALF = C // 2
+SLICES = ((0, 1), (1, 3), (3, 5), (5, 6))
 
 X_SPLIT = 512
-AHEAD = 7
+RAW = 8
+RAW_BYTES = PACK * H * 4
+ENGINE = "SSSSVSSVSVSVVSVVVL"
+BEHIND = (5, 8, 10, 13, 16)
 
 
 def tile_routed_moe_kernel(tc, xT, w1, w2, gate, offs, pos1, pos2, out):
     nc = tc.nc
     with ExitStack() as ctx:
         keep = ctx.enter_context(tc.tile_pool(name="keep", bufs=1))
+        raw_pool = ctx.enter_context(tc.tile_pool(name="raw_pool", bufs=1))
         xraw_pool = ctx.enter_context(tc.tile_pool(name="xraw_pool", bufs=3))
-        wraw_pool = ctx.enter_context(tc.tile_pool(name="wraw_pool", bufs=AHEAD + 1))
-        bf_pool = ctx.enter_context(tc.tile_pool(name="bf_pool", bufs=4))
         xbf_pool = ctx.enter_context(tc.tile_pool(name="xbf_pool", bufs=2))
-        code_pool = ctx.enter_context(tc.tile_pool(name="code_pool", bufs=6))
+        bf_pool = ctx.enter_context(tc.tile_pool(name="bf_pool", bufs=5))
+        code_pool = ctx.enter_context(tc.tile_pool(name="code_pool", bufs=9))
+        slot_pool = ctx.enter_context(tc.tile_pool(name="slot_pool", bufs=2))
         h_pool = ctx.enter_context(tc.tile_pool(name="h_pool", bufs=2))
-        psum = ctx.enter_context(tc.psum_pool(name="psum", bufs=2))
-        last_psum = ctx.enter_context(tc.psum_pool(name="last_psum", bufs=1))
+        end_pool = ctx.enter_context(tc.tile_pool(name="end_pool", bufs=1))
+        psum = ctx.enter_context(tc.psum_pool(name="psum", bufs=6))
+        y_psum = ctx.enter_context(tc.psum_pool(name="y_psum", bufs=2))
 
         offs_t = keep.tile([P, E * C // 16], U16, name="offs_t")
         pos_t = [keep.tile([P, T // 16], U16, name=f"pos_t{r}") for r in range(2)]
@@ -46,8 +50,6 @@ def tile_routed_moe_kernel(tc, xT, w1, w2, gate, offs, pos1, pos2, out):
         y_all = keep.tile([P, E * C], F32, name="y_all")
         tok_words = [keep.tile([P, T], U32, name=f"tok_words{g}", align_bytes=64) for g in range(PASSES)]
         tok_bytes = keep.tile([P, T], U8, name="tok_bytes", align_bytes=64)
-        slot_words = [[keep.tile([P, SLICE], U32, name=f"slot_words{s}_{g}", align_bytes=64) for g in range(PASSES)] for s in range(SLICES)]
-        slot_bytes = [keep.tile([P, SLICE], U8, name=f"slot_bytes{s}", align_bytes=64) for s in range(SLICES)]
         w2_raw = keep.tile([P, E, PACK, N], F32, name="w2_raw")
         w2_bf = keep.tile([P, E * N * PACK], BF16, name="w2_bf", align_bytes=64)
         w2_codes = keep.tile([P, E * N], U32, name="w2_codes", align_bytes=64)
@@ -63,12 +65,13 @@ def tile_routed_moe_kernel(tc, xT, w1, w2, gate, offs, pos1, pos2, out):
         for g in range(PASSES):
             x_raw.append(xraw_pool.tile([P, PACK, T], F32, name="x_raw"))
             src = xT[g * K_PASS : (g + 1) * K_PASS, :].rearrange("(p j) t -> p j t", j=PACK)
-            for cols in (slice(0, X_SPLIT), slice(X_SPLIT, T)) if g == 0 else (slice(0, T),):
+            for cols in (slice(0, 512), slice(512, T)) if g == 0 else (slice(0, T),):
                 nc.sync.dma_start(out=x_raw[g][:, :, cols], in_=src[:, :, cols])
             if g == 0:
                 nc.sync.dma_start(out=offs_t[:], in_=offs)
 
         chunks = [(e, g) for e in range(E) for g in range(PASSES)]
+        last = len(chunks) - 1
         w_raw = {}
 
         def load_w2(e0, e1):
@@ -76,9 +79,9 @@ def tile_routed_moe_kernel(tc, xT, w1, w2, gate, offs, pos1, pos2, out):
 
         def load(i):
             e, g = chunks[i]
-            w_raw[i] = wraw_pool.tile([P, PACK, H], F32, name="w_raw")
+            w_raw[i] = raw_pool.tile([P, PACK, H], F32, name=f"w_raw{i}", offset=i % RAW * RAW_BYTES, align_bytes=64)
             src = w1[e, g * K_PASS : (g + 1) * K_PASS, :].rearrange("(p j) h -> p j h", j=PACK)
-            if i < len(chunks) - 1:
+            if i < last:
                 nc.sync.dma_start(out=w_raw[i][:], in_=src)
             else:
                 for q in range(2):
@@ -93,7 +96,7 @@ def tile_routed_moe_kernel(tc, xT, w1, w2, gate, offs, pos1, pos2, out):
             if i == 14:
                 load_w2(4, 5)
 
-        for i in range(AHEAD):
+        for i in range(RAW):
             load(i)
 
         for g in range(PASSES):
@@ -110,47 +113,57 @@ def tile_routed_moe_kernel(tc, xT, w1, w2, gate, offs, pos1, pos2, out):
                     in_=x_bf[:, PACK * t0 : PACK * t1],
                 )
 
-        def gather_words(s, g):
-            nc.vector.tensor_copy(out=slot_words[s][g][:], in_=tok_words[g][:].indirect(offs_t[:, s * SLICE // 16 : (s + 1) * SLICE // 16]))
+        slot_words = {}
+        slot_bytes = {}
+        slice_of = {}
 
-        def gather_bytes(s):
-            nc.vector.tensor_copy(out=slot_bytes[s][:], in_=tok_bytes[:].indirect(offs_t[:, s * SLICE // 16 : (s + 1) * SLICE // 16]))
+        def gather(s):
+            e0, e1 = SLICES[s]
+            offsets = offs_t[:, e0 * C // 16 : e1 * C // 16]
+            for e in range(e0, e1):
+                slice_of[e] = (s, (e - e0) * C)
+            for g in range(PASSES):
+                slot_words[s, g] = slot_pool.tile([P, (e1 - e0) * C], U32, name=f"slot_words{g}", align_bytes=64)
+                nc.vector.tensor_copy(out=slot_words[s, g][:], in_=tok_words[g][:].indirect(offsets))
+            slot_bytes[s] = slot_pool.tile([P, (e1 - e0) * C], U8, name="slot_bytes", align_bytes=64)
+            nc.vector.tensor_copy(out=slot_bytes[s][:], in_=tok_bytes[:].indirect(offsets))
 
         w_bf = {}
         w_codes = {}
         w_scales = {}
 
+        def copy_on(engine, dst, src):
+            if engine == "V":
+                nc.vector.tensor_copy(out=dst, in_=src)
+            elif engine == "S":
+                nc.scalar.copy(out=dst, in_=src)
+            else:
+                nc.gpsimd.tensor_scalar(dst, src, 1.0, 0.0, MULT, ADD)
+
         def interleave(i):
             w_bf[i] = bf_pool.tile([P, H * PACK], BF16, name="w_bf", align_bytes=64)
             dst = w_bf[i][:].rearrange("p (t m j) -> p m j t", t=PACK, j=PACK)
             src = w_raw[i][:].rearrange("p j (m t) -> p m j t", t=PACK)
-            if i % PASSES == 1:
-                nc.vector.tensor_copy(out=dst, in_=src)
+            if ENGINE[i] == "L":
+                for q in range(2):
+                    m0 = 64 * q
+                    copy_on("S", dst[:, m0 : m0 + 24], src[:, m0 : m0 + 24])
+                    copy_on("V", dst[:, m0 + 24 : m0 + 64], src[:, m0 + 24 : m0 + 64])
+            elif ENGINE[i] == "G":
+                for q in range(4):
+                    copy_on("G", dst[:, 32 * q : 32 * q + 32], src[:, 32 * q : 32 * q + 32])
             else:
-                nc.scalar.copy(out=dst, in_=src)
-
-        def interleave_last(i):
-            w_bf[i] = bf_pool.tile([P, H * PACK], BF16, name="w_bf", align_bytes=64)
-            dst = w_bf[i][:].rearrange("p (t m j) -> p m j t", t=PACK, j=PACK)
-            src = w_raw[i][:].rearrange("p j (m t) -> p m j t", t=PACK)
-            for q in range(2):
-                m0 = 64 * q
-                nc.scalar.copy(out=dst[:, m0 : m0 + 24], in_=src[:, m0 : m0 + 24])
-                nc.vector.tensor_copy(out=dst[:, m0 + 24 : m0 + 64], in_=src[:, m0 + 24 : m0 + 64])
+                copy_on(ENGINE[i], dst, src)
 
         def quantize(i):
             w_codes[i] = code_pool.tile([P, H], U32, name="w_codes", align_bytes=64)
             w_scales[i] = code_pool.tile([P, H], U8, name="w_scales", align_bytes=64)
             nc.vector.quantize_mx(out=w_codes[i][:].bitcast(FP8X4), scales=w_scales[i][:], in_=w_bf[i][:])
 
-        def prepare_w2(e0, e1):
-            dst = w2_bf[:, e0 * N * PACK : e1 * N * PACK].rearrange("p (e c i j) -> p e c j i", c=N // 4, i=4, j=PACK)
-            src = w2_raw[:, e0:e1].rearrange("p e j (c i) -> p e c j i", i=4)
-            if e1 - e0 == 4:
-                nc.scalar.copy(out=dst[:, 0:2], in_=src[:, 0:2])
-                nc.vector.tensor_copy(out=dst[:, 2:4], in_=src[:, 2:4])
-            else:
-                nc.vector.tensor_copy(out=dst[:, 0], in_=src[:, 0])
+        def interleave_w2(e, engine):
+            dst = w2_bf[:, e * N * PACK : (e + 1) * N * PACK].rearrange("p (c i j) -> p c j i", i=4, j=PACK)
+            src = w2_raw[:, e].rearrange("p j (c i) -> p c j i", i=4)
+            copy_on(engine, dst, src)
 
         def quantize_w2(e0, e1):
             cols = slice(e0 * N, e1 * N)
@@ -162,14 +175,14 @@ def tile_routed_moe_kernel(tc, xT, w1, w2, gate, offs, pos1, pos2, out):
 
         def layer1_pass(acc, e, g, t, c0, c1):
             i = PASSES * e + g
-            s, base = divmod(e * C, SLICE)
+            s, base = slice_of[e]
             m_cols = slice(t * P, (t + 1) * P)
             n_cols = slice(base + c0, base + c1)
             nc.tensor.matmul_mx(
                 out=acc,
                 lhsT=w_codes[i][:, m_cols].bitcast(FP8X4),
                 lhsT_scale=w_scales[i][:, m_cols],
-                rhs=slot_words[s][g][:, n_cols].bitcast(FP8X4),
+                rhs=slot_words[s, g][:, n_cols].bitcast(FP8X4),
                 rhs_scale=slot_bytes[s][4 * g : P, n_cols],
                 start=(g == 0),
                 stop=(g == PASSES - 1),
@@ -185,8 +198,8 @@ def tile_routed_moe_kernel(tc, xT, w1, w2, gate, offs, pos1, pos2, out):
                 accs.append(acc)
             return accs
 
-        def silu(accs):
-            h_bf = h_pool.tile([P, C * PACK], BF16, name="h_bf", align_bytes=64)
+        def silu(e, accs):
+            h_bf = raw_pool.tile([P, C * PACK], BF16, name=f"h_bf{e}", offset=BEHIND[e] % RAW * RAW_BYTES, align_bytes=64)
             for half in range(2):
                 nc.scalar.activation(
                     h_bf[:, half * HALF * PACK : (half + 1) * HALF * PACK].rearrange("p (n t) -> p n t", t=PACK),
@@ -214,104 +227,77 @@ def tile_routed_moe_kernel(tc, xT, w1, w2, gate, offs, pos1, pos2, out):
                 stop=True,
             )
 
-        def hidden_codes(e):
-            hq[e] = quantize_h(h_bf[e])
-            if e > 0:
-                for d in (0, 1) if e == 1 else (e,):
-                    y_acc[d] = psum.tile([P, C], F32, name="y")
-                    layer2(y_acc[d][:], d, hq[d], 0, C)
-
-        def y_out(e):
-            if e > 0:
-                for d in (0, 1) if e == 1 else (e,):
-                    nc.scalar.copy(out=y_all[:, d * C : (d + 1) * C], in_=y_acc[d][:])
-
-        for g in range(PASSES):
-            gather_words(0, g)
-        gather_bytes(0)
-
-        pending = []
-        for s in range(1, SLICES):
-            for g in range(PASSES):
-                pending.append((s, g))
-            pending.append((s, PASSES))
-
-        h_bf = {}
-        hq = {}
-        y_acc = {}
+        gather(0)
+        gather(1)
         acc_of = {}
-        last = len(chunks) - 1
-        last_acc = [last_psum.tile([P, C], F32, name=f"last_acc{t}") for t in range(PACK)]
-        for i, (e, g) in enumerate(chunks):
-            if i + AHEAD <= last:
-                load(i + AHEAD)
-            if i < last:
-                interleave(i)
-            else:
-                interleave_last(i)
-            if g == 0 and e > 0:
-                quantize(i - 1)
-                if e > 1:
-                    hidden_codes(e - 2)
-                acc_of[e - 1] = layer1(e - 1)
-            if 1 <= i <= len(pending):
-                s, gg = pending[i - 1]
-                if gg < PASSES:
-                    gather_words(s, gg)
-                else:
-                    gather_bytes(s)
-            if g == 1:
-                quantize(i - 1)
-                quantize(i)
-            if g == 2 and e > 0:
-                y_out(e - 2)
-                h_bf[e - 1] = silu(acc_of[e - 1])
-            if i == 5:
-                prepare_w2(0, 4)
-                quantize_w2(0, 4)
-            if i == 14:
-                prepare_w2(4, 5)
-                quantize_w2(4, 5)
-            if i == last:
-                quantize(i)
-            if e == E - 1 and g > 0:
-                for gg in ((0, 1) if g == 1 else (2,)):
-                    for t in range(PACK):
-                        layer1_pass(last_acc[t][:], e, gg, t, 0, C)
-            if i == last:
-                hidden_codes(E - 2)
-                y_out(E - 2)
+        y_pair = [y_psum.tile([P, 2, C], F32, name="y_pair") for pair in range(2)]
 
-        prepare_w2(E - 1, E)
+        def finish(e):
+            h = quantize_h(silu(e, acc_of[e]))
+            if e < 4:
+                layer2(y_pair[e // 2][:, e % 2], e, h, 0, C)
+                if e % 2 == 1:
+                    nc.scalar.copy(out=y_all[:, (e - 1) * C : (e + 1) * C], in_=y_pair[e // 2][:].rearrange("p e n -> p (e n)"))
+            else:
+                y = psum.tile([P, C], F32, name="acc")
+                layer2(y[:], e, h, 0, C)
+                nc.scalar.copy(out=y_all[:, e * C : (e + 1) * C], in_=y[:])
+
+        last_acc = []
+        for i, (e, g) in enumerate(chunks):
+            interleave(i)
+            if i == 5:
+                for d in range(4):
+                    interleave_w2(d, "SSVV"[d])
+                quantize_w2(0, 4)
+            for b, behind in enumerate(BEHIND):
+                if i == behind:
+                    finish(b)
+            if i + RAW <= last:
+                load(i + RAW)
+            if i == 15:
+                interleave_w2(4, "V")
+                quantize_w2(4, 5)
+            quantize(i)
+            if e < E - 1 and g == PASSES - 1:
+                acc_of[e] = layer1(e)
+            if i == 3:
+                gather(2)
+            if i == 9:
+                gather(3)
+            if e == E - 1:
+                if g == 0:
+                    last_acc = [psum.tile([P, C], F32, name="acc") for t in range(PACK)]
+                for t in range(PACK):
+                    layer1_pass(last_acc[t][:], e, g, t, 0, C)
+
+        interleave_w2(E - 1, "V")
         quantize_w2(E - 1, E)
-        h_rows = h_pool.tile([P, PACK, C], BF16, name="h_rows")
+        h_rows = end_pool.tile([P, PACK, C], BF16, name="h_rows")
         for t in range(PACK):
             nc.scalar.activation(h_rows[:, t, :], last_acc[t][:], SILU)
-        h_last = h_pool.tile([P, C * PACK], BF16, name="h_bf", align_bytes=64)
+        h_last = end_pool.tile([P, C * PACK], BF16, name="h_last", align_bytes=64)
         nc.vector.tensor_copy(
             out=h_last[:].rearrange("p (c i t) -> p c t i", i=4, t=PACK),
             in_=h_rows[:].rearrange("p t (c i) -> p c t i", i=4),
         )
         h = quantize_h(h_last)
         for half in range(2):
-            y = psum.tile([P, C], F32, name="y")
+            y = psum.tile([P, C], F32, name="acc")
             layer2(y[:, :HALF], E - 1, h, half * HALF, (half + 1) * HALF)
             dst = y_all[:, (E - 1) * C + half * HALF : (E - 1) * C + (half + 1) * HALF]
-            if half == 0:
-                nc.vector.tensor_copy(out=dst, in_=y[:, :HALF])
-            else:
-                nc.scalar.copy(out=dst, in_=y[:, :HALF])
+            copy_on("VS"[half], dst, y[:, :HALF])
 
         for t0, t1 in ((0, 512), (512, T)):
             cols = slice(t0, t1)
-            part = [h_pool.tile([P, 512], F32, name=f"part{r}") for r in range(2)]
+            part = [end_pool.tile([P, t1 - t0], F32, name=f"part{r}_{t0}") for r in range(2)]
             for r in range(2):
                 nc.vector.tensor_tensor(
-                    part[r][:, : t1 - t0],
+                    part[r][:],
                     y_all[:].indirect(pos_t[r][:, t0 // 16 : t1 // 16]),
                     gate_t[:, r, cols],
                     MULT,
                 )
-            total = h_pool.tile([P, 512], F32, name="total")
-            nc.vector.tensor_tensor(total[:, : t1 - t0], part[0][:, : t1 - t0], part[1][:, : t1 - t0], ADD)
-            nc.sync.dma_start(out=out[:, cols], in_=total[:, : t1 - t0])
+            total = end_pool.tile([P, t1 - t0], F32, name=f"total_{t0}")
+            nc.vector.tensor_tensor(total[:], part[0][:], part[1][:], ADD)
+            nc.sync.dma_start(out=out[:, cols], in_=total[:])

@@ -22,11 +22,16 @@ PASSES = K // K_PASS
 HALF = C // 2
 SLICES = ((0, 1), (1, 3), (3, 5), (5, 6))
 
-X_SPLIT = 512
-RAW = 8
+X_SPLIT = 256
+RAW = 9
+X_RAW_BYTES = PACK * T * 4
+X_AREA = PASSES * X_RAW_BYTES
+RAW_BEHIND_X = 5
+W2E = "VVSVSV"
+YE = "SSS"
 RAW_BYTES = PACK * H * 4
-ENGINE = "SSSSVSSVSVSVVSVVVL"
-BEHIND = (5, 8, 10, 13, 16)
+ENGINE = "SSSVSSSVSVVVSVSVSL"
+BEHIND = (5, 9, 10, 12, 16)
 
 
 def tile_routed_moe_kernel(tc, xT, w1, w2, gate, offs, pos1, pos2, out):
@@ -34,12 +39,12 @@ def tile_routed_moe_kernel(tc, xT, w1, w2, gate, offs, pos1, pos2, out):
     with ExitStack() as ctx:
         keep = ctx.enter_context(tc.tile_pool(name="keep", bufs=1))
         raw_pool = ctx.enter_context(tc.tile_pool(name="raw_pool", bufs=1))
-        xraw_pool = ctx.enter_context(tc.tile_pool(name="xraw_pool", bufs=3))
         xbf_pool = ctx.enter_context(tc.tile_pool(name="xbf_pool", bufs=2))
-        bf_pool = ctx.enter_context(tc.tile_pool(name="bf_pool", bufs=5))
-        code_pool = ctx.enter_context(tc.tile_pool(name="code_pool", bufs=9))
+        pair_pool = ctx.enter_context(tc.tile_pool(name="pair_pool", bufs=3))
+        bf_pool = ctx.enter_context(tc.tile_pool(name="bf_pool", bufs=3))
+        code_pool = ctx.enter_context(tc.tile_pool(name="code_pool", bufs=3))
         slot_pool = ctx.enter_context(tc.tile_pool(name="slot_pool", bufs=2))
-        h_pool = ctx.enter_context(tc.tile_pool(name="h_pool", bufs=2))
+        h_pool = ctx.enter_context(tc.tile_pool(name="h_pool", bufs=6))
         end_pool = ctx.enter_context(tc.tile_pool(name="end_pool", bufs=1))
         psum = ctx.enter_context(tc.psum_pool(name="psum", bufs=6))
         y_psum = ctx.enter_context(tc.psum_pool(name="y_psum", bufs=2))
@@ -63,9 +68,9 @@ def tile_routed_moe_kernel(tc, xT, w1, w2, gate, offs, pos1, pos2, out):
 
         x_raw = []
         for g in range(PASSES):
-            x_raw.append(xraw_pool.tile([P, PACK, T], F32, name="x_raw"))
+            x_raw.append(raw_pool.tile([P, PACK, T], F32, name=f"x_raw{g}", offset=g * X_RAW_BYTES, align_bytes=64))
             src = xT[g * K_PASS : (g + 1) * K_PASS, :].rearrange("(p j) t -> p j t", j=PACK)
-            for cols in (slice(0, 512), slice(512, T)) if g == 0 else (slice(0, T),):
+            for cols in (slice(0, X_SPLIT), slice(X_SPLIT, T)) if g == 0 else (slice(0, T),):
                 nc.sync.dma_start(out=x_raw[g][:, :, cols], in_=src[:, :, cols])
             if g == 0:
                 nc.sync.dma_start(out=offs_t[:], in_=offs)
@@ -74,12 +79,16 @@ def tile_routed_moe_kernel(tc, xT, w1, w2, gate, offs, pos1, pos2, out):
         last = len(chunks) - 1
         w_raw = {}
 
+        def raw_place(i):
+            slot = i % RAW
+            return X_AREA + slot * RAW_BYTES if slot < RAW_BEHIND_X else (slot - RAW_BEHIND_X) * RAW_BYTES
+
         def load_w2(e0, e1):
             nc.sync.dma_start(out=w2_raw[:, e0:e1], in_=w2[e0:e1].rearrange("e (p j) n -> p e j n", j=PACK))
 
         def load(i):
             e, g = chunks[i]
-            w_raw[i] = raw_pool.tile([P, PACK, H], F32, name=f"w_raw{i}", offset=i % RAW * RAW_BYTES, align_bytes=64)
+            w_raw[i] = raw_pool.tile([P, PACK, H], F32, name=f"w_raw{i}", offset=raw_place(i), align_bytes=64)
             src = w1[e, g * K_PASS : (g + 1) * K_PASS, :].rearrange("(p j) h -> p j h", j=PACK)
             if i < last:
                 nc.sync.dma_start(out=w_raw[i][:], in_=src)
@@ -87,16 +96,13 @@ def tile_routed_moe_kernel(tc, xT, w1, w2, gate, offs, pos1, pos2, out):
                 for q in range(2):
                     cols = slice(q * H // 2, (q + 1) * H // 2)
                     nc.sync.dma_start(out=w_raw[i][:, :, cols], in_=src[:, :, cols])
-                load_w2(E - 1, E)
+                for e0 in (0, 2, 4):
+                    load_w2(e0, e0 + 2)
                 for r, pos in enumerate((pos1, pos2)):
                     nc.sync.dma_start(out=pos_t[r][:], in_=pos)
                 nc.sync.dma_start(out=gate_t[:], in_=gate.rearrange("r p t -> p r t"))
-            if i == 4:
-                load_w2(0, 4)
-            if i == 14:
-                load_w2(4, 5)
 
-        for i in range(RAW):
+        for i in range(RAW_BEHIND_X):
             load(i)
 
         for g in range(PASSES):
@@ -104,14 +110,18 @@ def tile_routed_moe_kernel(tc, xT, w1, w2, gate, offs, pos1, pos2, out):
             dst = x_bf[:].rearrange("p (c i j) -> p c j i", i=4, j=PACK)
             src = x_raw[g][:].rearrange("p j (c i) -> p c j i", i=4)
             split = X_SPLIT // 4
-            nc.vector.tensor_copy(out=dst[:, :split], in_=src[:, :split])
-            nc.scalar.copy(out=dst[:, split:], in_=src[:, split:])
-            for t0, t1 in ((0, 512), (512, T)):
+            first, second = (nc.vector.tensor_copy,) * 2 if g == 0 else (nc.vector.tensor_copy, nc.scalar.copy)
+            first(out=dst[:, :split], in_=src[:, :split])
+            second(out=dst[:, split:], in_=src[:, split:])
+            for t0, t1 in ((0, X_SPLIT), (X_SPLIT, T)):
                 nc.vector.quantize_mx(
                     out=tok_words[g][:, t0:t1].bitcast(FP8X4),
                     scales=tok_bytes[4 * g : P, t0:t1],
                     in_=x_bf[:, PACK * t0 : PACK * t1],
                 )
+
+        for i in range(RAW_BEHIND_X, RAW):
+            load(i)
 
         slot_words = {}
         slot_bytes = {}
@@ -141,8 +151,14 @@ def tile_routed_moe_kernel(tc, xT, w1, w2, gate, offs, pos1, pos2, out):
                 nc.gpsimd.tensor_scalar(dst, src, 1.0, 0.0, MULT, ADD)
 
         def interleave(i):
-            w_bf[i] = bf_pool.tile([P, H * PACK], BF16, name="w_bf", align_bytes=64)
-            dst = w_bf[i][:].rearrange("p (t m j) -> p m j t", t=PACK, j=PACK)
+            g = i % PASSES
+            if g == 0:
+                w_bf[i] = pair_pool.tile([P, 2, H * PACK], BF16, name="w_bf_pair", align_bytes=64)
+            elif g == 1:
+                w_bf[i] = w_bf[i - 1]
+            else:
+                w_bf[i] = bf_pool.tile([P, 1, H * PACK], BF16, name="w_bf", align_bytes=64)
+            dst = w_bf[i][:, g % 2].rearrange("p (t m j) -> p m j t", t=PACK, j=PACK)
             src = w_raw[i][:].rearrange("p j (m t) -> p m j t", t=PACK)
             if ENGINE[i] == "L":
                 for q in range(2):
@@ -156,9 +172,23 @@ def tile_routed_moe_kernel(tc, xT, w1, w2, gate, offs, pos1, pos2, out):
                 copy_on(ENGINE[i], dst, src)
 
         def quantize(i):
-            w_codes[i] = code_pool.tile([P, H], U32, name="w_codes", align_bytes=64)
-            w_scales[i] = code_pool.tile([P, H], U8, name="w_scales", align_bytes=64)
-            nc.vector.quantize_mx(out=w_codes[i][:].bitcast(FP8X4), scales=w_scales[i][:], in_=w_bf[i][:])
+            if i % PASSES == 0:
+                return
+            n = 2 if i % PASSES == 1 else 1
+            codes = code_pool.tile([P, n * H], U32, name=f"w_codes{n}", align_bytes=64)
+            scales = code_pool.tile([P, n * H], U8, name=f"w_scales{n}", align_bytes=64)
+            for k in range(n):
+                w_codes[i - n + 1 + k] = codes[:, k * H : (k + 1) * H]
+                w_scales[i - n + 1 + k] = scales[:, k * H : (k + 1) * H]
+            parts = 2 if i == last else 1
+            flat = w_bf[i][:].rearrange("p g n -> p (g n)")
+            for q in range(parts):
+                cols = slice(q * n * H // parts, (q + 1) * n * H // parts)
+                nc.vector.quantize_mx(
+                    out=codes[:, cols].bitcast(FP8X4),
+                    scales=scales[:, cols],
+                    in_=flat[:, q * n * H * PACK // parts : (q + 1) * n * H * PACK // parts],
+                )
 
         def interleave_w2(e, engine):
             dst = w2_bf[:, e * N * PACK : (e + 1) * N * PACK].rearrange("p (c i j) -> p c j i", i=4, j=PACK)
@@ -199,7 +229,7 @@ def tile_routed_moe_kernel(tc, xT, w1, w2, gate, offs, pos1, pos2, out):
             return accs
 
         def silu(e, accs):
-            h_bf = raw_pool.tile([P, C * PACK], BF16, name=f"h_bf{e}", offset=BEHIND[e] % RAW * RAW_BYTES, align_bytes=64)
+            h_bf = raw_pool.tile([P, C * PACK], BF16, name=f"h_bf{e}", offset=raw_place(BEHIND[e]), align_bytes=64)
             for half in range(2):
                 nc.scalar.activation(
                     h_bf[:, half * HALF * PACK : (half + 1) * HALF * PACK].rearrange("p (n t) -> p n t", t=PACK),
@@ -230,34 +260,20 @@ def tile_routed_moe_kernel(tc, xT, w1, w2, gate, offs, pos1, pos2, out):
         gather(0)
         gather(1)
         acc_of = {}
-        y_pair = [y_psum.tile([P, 2, C], F32, name="y_pair") for pair in range(2)]
+
+        h_of = {}
 
         def finish(e):
-            h = quantize_h(silu(e, acc_of[e]))
-            if e < 4:
-                layer2(y_pair[e // 2][:, e % 2], e, h, 0, C)
-                if e % 2 == 1:
-                    nc.scalar.copy(out=y_all[:, (e - 1) * C : (e + 1) * C], in_=y_pair[e // 2][:].rearrange("p e n -> p (e n)"))
-            else:
-                y = psum.tile([P, C], F32, name="acc")
-                layer2(y[:], e, h, 0, C)
-                nc.scalar.copy(out=y_all[:, e * C : (e + 1) * C], in_=y[:])
+            h_of[e] = quantize_h(silu(e, acc_of[e]))
 
         last_acc = []
         for i, (e, g) in enumerate(chunks):
             interleave(i)
-            if i == 5:
-                for d in range(4):
-                    interleave_w2(d, "SSVV"[d])
-                quantize_w2(0, 4)
             for b, behind in enumerate(BEHIND):
                 if i == behind:
                     finish(b)
             if i + RAW <= last:
                 load(i + RAW)
-            if i == 15:
-                interleave_w2(4, "V")
-                quantize_w2(4, 5)
             quantize(i)
             if e < E - 1 and g == PASSES - 1:
                 acc_of[e] = layer1(e)
@@ -268,25 +284,35 @@ def tile_routed_moe_kernel(tc, xT, w1, w2, gate, offs, pos1, pos2, out):
             if e == E - 1:
                 if g == 0:
                     last_acc = [psum.tile([P, C], F32, name="acc") for t in range(PACK)]
-                for t in range(PACK):
-                    layer1_pass(last_acc[t][:], e, g, t, 0, C)
+                for gg in ((), (0, 1), (2,))[g]:
+                    for t in range(PACK):
+                        layer1_pass(last_acc[t][:], e, gg, t, 0, C)
 
-        interleave_w2(E - 1, "V")
-        quantize_w2(E - 1, E)
         h_rows = end_pool.tile([P, PACK, C], BF16, name="h_rows")
         for t in range(PACK):
             nc.scalar.activation(h_rows[:, t, :], last_acc[t][:], SILU)
+        for e0 in (0, 2, 4):
+            for d in (e0, e0 + 1):
+                interleave_w2(d, W2E[d])
+            quantize_w2(e0, e0 + 2)
+            if e0 < 4:
+                y = y_psum.tile([P, 2, C], F32, name="y_pair")
+                for d in (e0, e0 + 1):
+                    layer2(y[:, d - e0], d, h_of[d], 0, C)
+                copy_on(YE[e0 // 2], y_all[:, e0 * C : (e0 + 2) * C], y[:].rearrange("p e n -> p (e n)"))
+            else:
+                y = psum.tile([P, C], F32, name="acc")
+                layer2(y[:], 4, h_of[4], 0, C)
+                copy_on(YE[2], y_all[:, 4 * C : 5 * C], y[:])
         h_last = end_pool.tile([P, C * PACK], BF16, name="h_last", align_bytes=64)
         nc.vector.tensor_copy(
             out=h_last[:].rearrange("p (c i t) -> p c t i", i=4, t=PACK),
             in_=h_rows[:].rearrange("p t (c i) -> p c t i", i=4),
         )
         h = quantize_h(h_last)
-        for half in range(2):
-            y = psum.tile([P, C], F32, name="acc")
-            layer2(y[:, :HALF], E - 1, h, half * HALF, (half + 1) * HALF)
-            dst = y_all[:, (E - 1) * C + half * HALF : (E - 1) * C + (half + 1) * HALF]
-            copy_on("VS"[half], dst, y[:, :HALF])
+        y = psum.tile([P, C], F32, name="acc")
+        layer2(y[:], E - 1, h, 0, C)
+        nc.vector.tensor_copy(out=y_all[:, (E - 1) * C :], in_=y[:])
 
         for t0, t1 in ((0, 512), (512, T)):
             cols = slice(t0, t1)

@@ -20,18 +20,25 @@ PACK = 4
 K_PASS = P * PACK
 PASSES = K // K_PASS
 HALF = C // 2
-SLICES = ((0, 1), (1, 3), (3, 5), (5, 6))
+SLICES = ((0, 2), (2, 4), (4, 6))
 
 X_SPLIT = 256
+X_ENGINE = 'SVVSVS'
+M_CUT = 88
+L_CUT = 16
+GATHER_AT = (6,)
+DEPTHS = (3, 3, 3)
+BACK = (576, 192)
 RAW = 9
 X_RAW_BYTES = PACK * T * 4
 X_AREA = PASSES * X_RAW_BYTES
 RAW_BEHIND_X = 5
-W2E = "VVSVSV"
-YE = "SSS"
+W2_AT = (16, 17, 17)
+W2E = 'VVSVVS'
+YE = 'SVV'
 RAW_BYTES = PACK * H * 4
-ENGINE = "SSSVSSSVSVVVSVSVSL"
-BEHIND = (5, 9, 10, 12, 16)
+ENGINE = 'VSSSVSSVSSVSSVSVSL'
+BEHIND = (5, 8, 11, 14, 16)
 
 
 def tile_routed_moe_kernel(tc, xT, w1, w2, gate, offs, pos1, pos2, out):
@@ -40,9 +47,9 @@ def tile_routed_moe_kernel(tc, xT, w1, w2, gate, offs, pos1, pos2, out):
         keep = ctx.enter_context(tc.tile_pool(name="keep", bufs=1))
         raw_pool = ctx.enter_context(tc.tile_pool(name="raw_pool", bufs=1))
         xbf_pool = ctx.enter_context(tc.tile_pool(name="xbf_pool", bufs=2))
-        pair_pool = ctx.enter_context(tc.tile_pool(name="pair_pool", bufs=3))
-        bf_pool = ctx.enter_context(tc.tile_pool(name="bf_pool", bufs=3))
-        code_pool = ctx.enter_context(tc.tile_pool(name="code_pool", bufs=3))
+        pair_pool = ctx.enter_context(tc.tile_pool(name="pair_pool", bufs=DEPTHS[0]))
+        bf_pool = ctx.enter_context(tc.tile_pool(name="bf_pool", bufs=DEPTHS[1]))
+        code_pool = ctx.enter_context(tc.tile_pool(name="code_pool", bufs=DEPTHS[2]))
         slot_pool = ctx.enter_context(tc.tile_pool(name="slot_pool", bufs=2))
         h_pool = ctx.enter_context(tc.tile_pool(name="h_pool", bufs=6))
         end_pool = ctx.enter_context(tc.tile_pool(name="end_pool", bufs=1))
@@ -65,6 +72,12 @@ def tile_routed_moe_kernel(tc, xT, w1, w2, gate, offs, pos1, pos2, out):
         nc.gpsimd.memset(zero[:], 0.0)
         nc.scalar.activation(silu_zero[:], zero[:], SILU)
         nc.gpsimd.memset(tok_bytes[:], 0)
+
+        def copy_on(engine, dst, src):
+            if engine == "V":
+                nc.vector.tensor_copy(out=dst, in_=src)
+            else:
+                nc.scalar.copy(out=dst, in_=src)
 
         x_raw = []
         for g in range(PASSES):
@@ -96,8 +109,10 @@ def tile_routed_moe_kernel(tc, xT, w1, w2, gate, offs, pos1, pos2, out):
                 for q in range(2):
                     cols = slice(q * H // 2, (q + 1) * H // 2)
                     nc.sync.dma_start(out=w_raw[i][:, :, cols], in_=src[:, :, cols])
-                for e0 in (0, 2, 4):
-                    load_w2(e0, e0 + 2)
+            for pair, at in enumerate(W2_AT):
+                if i == at:
+                    load_w2(2 * pair, 2 * pair + 2)
+            if i == last:
                 for r, pos in enumerate((pos1, pos2)):
                     nc.sync.dma_start(out=pos_t[r][:], in_=pos)
                 nc.sync.dma_start(out=gate_t[:], in_=gate.rearrange("r p t -> p r t"))
@@ -110,9 +125,8 @@ def tile_routed_moe_kernel(tc, xT, w1, w2, gate, offs, pos1, pos2, out):
             dst = x_bf[:].rearrange("p (c i j) -> p c j i", i=4, j=PACK)
             src = x_raw[g][:].rearrange("p j (c i) -> p c j i", i=4)
             split = X_SPLIT // 4
-            first, second = (nc.vector.tensor_copy,) * 2 if g == 0 else (nc.vector.tensor_copy, nc.scalar.copy)
-            first(out=dst[:, :split], in_=src[:, :split])
-            second(out=dst[:, split:], in_=src[:, split:])
+            copy_on(X_ENGINE[2 * g], dst[:, :split], src[:, :split])
+            copy_on(X_ENGINE[2 * g + 1], dst[:, split:], src[:, split:])
             for t0, t1 in ((0, X_SPLIT), (X_SPLIT, T)):
                 nc.vector.quantize_mx(
                     out=tok_words[g][:, t0:t1].bitcast(FP8X4),
@@ -142,14 +156,6 @@ def tile_routed_moe_kernel(tc, xT, w1, w2, gate, offs, pos1, pos2, out):
         w_codes = {}
         w_scales = {}
 
-        def copy_on(engine, dst, src):
-            if engine == "V":
-                nc.vector.tensor_copy(out=dst, in_=src)
-            elif engine == "S":
-                nc.scalar.copy(out=dst, in_=src)
-            else:
-                nc.gpsimd.tensor_scalar(dst, src, 1.0, 0.0, MULT, ADD)
-
         def interleave(i):
             g = i % PASSES
             if g == 0:
@@ -163,11 +169,11 @@ def tile_routed_moe_kernel(tc, xT, w1, w2, gate, offs, pos1, pos2, out):
             if ENGINE[i] == "L":
                 for q in range(2):
                     m0 = 64 * q
-                    copy_on("S", dst[:, m0 : m0 + 24], src[:, m0 : m0 + 24])
-                    copy_on("V", dst[:, m0 + 24 : m0 + 64], src[:, m0 + 24 : m0 + 64])
-            elif ENGINE[i] == "G":
-                for q in range(4):
-                    copy_on("G", dst[:, 32 * q : 32 * q + 32], src[:, 32 * q : 32 * q + 32])
+                    copy_on("S", dst[:, m0 : m0 + L_CUT], src[:, m0 : m0 + L_CUT])
+                    copy_on("V", dst[:, m0 + L_CUT : m0 + 64], src[:, m0 + L_CUT : m0 + 64])
+            elif ENGINE[i] == "M":
+                copy_on("S", dst[:, :M_CUT], src[:, :M_CUT])
+                copy_on("V", dst[:, M_CUT:], src[:, M_CUT:])
             else:
                 copy_on(ENGINE[i], dst, src)
 
@@ -259,6 +265,23 @@ def tile_routed_moe_kernel(tc, xT, w1, w2, gate, offs, pos1, pos2, out):
 
         gather(0)
         gather(1)
+        def prepare_w2(pair):
+            for d in (2 * pair, 2 * pair + 1):
+                interleave_w2(d, W2E[d])
+            quantize_w2(2 * pair, 2 * pair + 2)
+
+        def results(pair):
+            e0 = 2 * pair
+            if pair < 2:
+                y = y_psum.tile([P, 2, C], F32, name="y_pair")
+                for d in (e0, e0 + 1):
+                    layer2(y[:, d - e0], d, h_of[d], 0, C)
+                copy_on(YE[pair], y_all[:, e0 * C : (e0 + 2) * C], y[:].rearrange("p e n -> p (e n)"))
+            else:
+                y = psum.tile([P, C], F32, name="acc")
+                layer2(y[:], 4, h_of[4], 0, C)
+                copy_on(YE[2], y_all[:, 4 * C : 5 * C], y[:])
+
         acc_of = {}
 
         h_of = {}
@@ -269,18 +292,23 @@ def tile_routed_moe_kernel(tc, xT, w1, w2, gate, offs, pos1, pos2, out):
         last_acc = []
         for i, (e, g) in enumerate(chunks):
             interleave(i)
+            for pair, at in enumerate(W2_AT):
+                if i == at + 1:
+                    prepare_w2(pair)
             for b, behind in enumerate(BEHIND):
                 if i == behind:
                     finish(b)
+            for pair, at in enumerate(W2_AT):
+                if i == max(at + 1, BEHIND[min(2 * pair + 1, 4)]):
+                    results(pair)
             if i + RAW <= last:
                 load(i + RAW)
             quantize(i)
             if e < E - 1 and g == PASSES - 1:
                 acc_of[e] = layer1(e)
-            if i == 3:
-                gather(2)
-            if i == 9:
-                gather(3)
+            for k, at in enumerate(GATHER_AT):
+                if i == at:
+                    gather(2 + k)
             if e == E - 1:
                 if g == 0:
                     last_acc = [psum.tile([P, C], F32, name="acc") for t in range(PACK)]
@@ -291,19 +319,10 @@ def tile_routed_moe_kernel(tc, xT, w1, w2, gate, offs, pos1, pos2, out):
         h_rows = end_pool.tile([P, PACK, C], BF16, name="h_rows")
         for t in range(PACK):
             nc.scalar.activation(h_rows[:, t, :], last_acc[t][:], SILU)
-        for e0 in (0, 2, 4):
-            for d in (e0, e0 + 1):
-                interleave_w2(d, W2E[d])
-            quantize_w2(e0, e0 + 2)
-            if e0 < 4:
-                y = y_psum.tile([P, 2, C], F32, name="y_pair")
-                for d in (e0, e0 + 1):
-                    layer2(y[:, d - e0], d, h_of[d], 0, C)
-                copy_on(YE[e0 // 2], y_all[:, e0 * C : (e0 + 2) * C], y[:].rearrange("p e n -> p (e n)"))
-            else:
-                y = psum.tile([P, C], F32, name="acc")
-                layer2(y[:], 4, h_of[4], 0, C)
-                copy_on(YE[2], y_all[:, 4 * C : 5 * C], y[:])
+        for pair in range(3):
+            if W2_AT[pair] == last:
+                prepare_w2(pair)
+                results(pair)
         h_last = end_pool.tile([P, C * PACK], BF16, name="h_last", align_bytes=64)
         nc.vector.tensor_copy(
             out=h_last[:].rearrange("p (c i t) -> p c t i", i=4, t=PACK),
@@ -314,7 +333,9 @@ def tile_routed_moe_kernel(tc, xT, w1, w2, gate, offs, pos1, pos2, out):
         layer2(y[:], E - 1, h, 0, C)
         nc.vector.tensor_copy(out=y_all[:, (E - 1) * C :], in_=y[:])
 
-        for t0, t1 in ((0, 512), (512, T)):
+        for back in range(len(BACK)):
+            t0 = sum(BACK[:back])
+            t1 = t0 + BACK[back]
             cols = slice(t0, t1)
             part = [end_pool.tile([P, t1 - t0], F32, name=f"part{r}_{t0}") for r in range(2)]
             for r in range(2):

from contextlib import ExitStack

import concourse.mybir as mybir

K, T, E, C, H, N = 1536, 768, 6, 256, 512, 128
FLOPS = 2 * E * C * (K * H + H * N)

F32 = mybir.dt.float32
BF16 = mybir.dt.bfloat16
U32 = mybir.dt.uint32
U16 = mybir.dt.uint16
U8 = mybir.dt.uint8
FP8X4 = mybir.dt.float8_e4m3fn_x4
SILU = mybir.ActivationFunctionType.Silu
MULT = mybir.AluOpType.mult
ADD = mybir.AluOpType.add

P = 128
PACK = 4
K_PASS = P * PACK
PASSES = K // K_PASS
HALF = C // 2
SLICES = ((0, 2), (2, 4), (4, 6))

X_SPLIT = 256
X_ENGINE = 'SVVSVS'
M_CUT = 88
L_CUT = 16
GATHER_AT = (6,)
DEPTHS = (3, 3, 3)
BACK = (576, 192)
RAW = 9
X_RAW_BYTES = PACK * T * 4
X_AREA = PASSES * X_RAW_BYTES
RAW_BEHIND_X = 5
W2_AT = (16, 17, 17)
W2E = 'VVSVVS'
YE = 'SVV'
RAW_BYTES = PACK * H * 4
ENGINE = 'VSSSVSSVSSVSSVSVSL'
BEHIND = (5, 8, 11, 14, 16)


def tile_routed_moe_kernel(tc, xT, w1, w2, gate, offs, pos1, pos2, out):
    nc = tc.nc
    with ExitStack() as ctx:
        keep = ctx.enter_context(tc.tile_pool(name="keep", bufs=1))
        raw_pool = ctx.enter_context(tc.tile_pool(name="raw_pool", bufs=1))
        xbf_pool = ctx.enter_context(tc.tile_pool(name="xbf_pool", bufs=2))
        pair_pool = ctx.enter_context(tc.tile_pool(name="pair_pool", bufs=DEPTHS[0]))
        bf_pool = ctx.enter_context(tc.tile_pool(name="bf_pool", bufs=DEPTHS[1]))
        code_pool = ctx.enter_context(tc.tile_pool(name="code_pool", bufs=DEPTHS[2]))
        slot_pool = ctx.enter_context(tc.tile_pool(name="slot_pool", bufs=2))
        h_pool = ctx.enter_context(tc.tile_pool(name="h_pool", bufs=6))
        end_pool = ctx.enter_context(tc.tile_pool(name="end_pool", bufs=1))
        psum = ctx.enter_context(tc.psum_pool(name="psum", bufs=6))
        y_psum = ctx.enter_context(tc.psum_pool(name="y_psum", bufs=2))

        offs_t = keep.tile([P, E * C // 16], U16, name="offs_t")
        pos_t = [keep.tile([P, T // 16], U16, name=f"pos_t{r}") for r in range(2)]
        gate_t = keep.tile([P, 2, T], F32, name="gate_t")
        y_all = keep.tile([P, E * C], F32, name="y_all")
        tok_words = [keep.tile([P, T], U32, name=f"tok_words{g}", align_bytes=64) for g in range(PASSES)]
        tok_bytes = keep.tile([P, T], U8, name="tok_bytes", align_bytes=64)
        w2_raw = keep.tile([P, E, PACK, N], F32, name="w2_raw")
        w2_bf = keep.tile([P, E * N * PACK], BF16, name="w2_bf", align_bytes=64)
        w2_codes = keep.tile([P, E * N], U32, name="w2_codes", align_bytes=64)
        w2_scales = keep.tile([P, E * N], U8, name="w2_scales", align_bytes=64)
        zero = keep.tile([P, 1], F32, name="zero")
        silu_zero = keep.tile([P, 1], F32, name="silu_zero")

        nc.gpsimd.memset(zero[:], 0.0)
        nc.scalar.activation(silu_zero[:], zero[:], SILU)
        nc.gpsimd.memset(tok_bytes[:], 0)

        def copy_on(engine, dst, src):
            if engine == "V":
                nc.vector.tensor_copy(out=dst, in_=src)
            else:
                nc.scalar.copy(out=dst, in_=src)

        x_raw = []
        for g in range(PASSES):
            x_raw.append(raw_pool.tile([P, PACK, T], F32, name=f"x_raw{g}", offset=g * X_RAW_BYTES, align_bytes=64))
            src = xT[g * K_PASS : (g + 1) * K_PASS, :].rearrange("(p j) t -> p j t", j=PACK)
            for cols in (slice(0, X_SPLIT), slice(X_SPLIT, T)) if g == 0 else (slice(0, T),):
                nc.sync.dma_start(out=x_raw[g][:, :, cols], in_=src[:, :, cols])
            if g == 0:
                nc.sync.dma_start(out=offs_t[:], in_=offs)

        chunks = [(e, g) for e in range(E) for g in range(PASSES)]
        last = len(chunks) - 1
        w_raw = {}

        def raw_place(i):
            slot = i % RAW
            return X_AREA + slot * RAW_BYTES if slot < RAW_BEHIND_X else (slot - RAW_BEHIND_X) * RAW_BYTES

        def load_w2(e0, e1):
            nc.sync.dma_start(out=w2_raw[:, e0:e1], in_=w2[e0:e1].rearrange("e (p j) n -> p e j n", j=PACK))

        def load(i):
            e, g = chunks[i]
            w_raw[i] = raw_pool.tile([P, PACK, H], F32, name=f"w_raw{i}", offset=raw_place(i), align_bytes=64)
            src = w1[e, g * K_PASS : (g + 1) * K_PASS, :].rearrange("(p j) h -> p j h", j=PACK)
            if i < last:
                nc.sync.dma_start(out=w_raw[i][:], in_=src)
            else:
                for q in range(2):
                    cols = slice(q * H // 2, (q + 1) * H // 2)
                    nc.sync.dma_start(out=w_raw[i][:, :, cols], in_=src[:, :, cols])
            for pair, at in enumerate(W2_AT):
                if i == at:
                    load_w2(2 * pair, 2 * pair + 2)
            if i == last:
                for r, pos in enumerate((pos1, pos2)):
                    nc.sync.dma_start(out=pos_t[r][:], in_=pos)
                nc.sync.dma_start(out=gate_t[:], in_=gate.rearrange("r p t -> p r t"))

        for i in range(RAW_BEHIND_X):
            load(i)

        for g in range(PASSES):
            x_bf = xbf_pool.tile([P, T * PACK], BF16, name="x_bf", align_bytes=64)
            dst = x_bf[:].rearrange("p (c i j) -> p c j i", i=4, j=PACK)
            src = x_raw[g][:].rearrange("p j (c i) -> p c j i", i=4)
            split = X_SPLIT // 4
            copy_on(X_ENGINE[2 * g], dst[:, :split], src[:, :split])
            copy_on(X_ENGINE[2 * g + 1], dst[:, split:], src[:, split:])
            for t0, t1 in ((0, X_SPLIT), (X_SPLIT, T)):
                nc.vector.quantize_mx(
                    out=tok_words[g][:, t0:t1].bitcast(FP8X4),
                    scales=tok_bytes[4 * g : P, t0:t1],
                    in_=x_bf[:, PACK * t0 : PACK * t1],
                )

        for i in range(RAW_BEHIND_X, RAW):
            load(i)

        slot_words = {}
        slot_bytes = {}
        slice_of = {}

        def gather(s):
            e0, e1 = SLICES[s]
            offsets = offs_t[:, e0 * C // 16 : e1 * C // 16]
            for e in range(e0, e1):
                slice_of[e] = (s, (e - e0) * C)
            for g in range(PASSES):
                slot_words[s, g] = slot_pool.tile([P, (e1 - e0) * C], U32, name=f"slot_words{g}", align_bytes=64)
                nc.vector.tensor_copy(out=slot_words[s, g][:], in_=tok_words[g][:].indirect(offsets))
            slot_bytes[s] = slot_pool.tile([P, (e1 - e0) * C], U8, name="slot_bytes", align_bytes=64)
            nc.vector.tensor_copy(out=slot_bytes[s][:], in_=tok_bytes[:].indirect(offsets))

        w_bf = {}
        w_codes = {}
        w_scales = {}

        def interleave(i):
            g = i % PASSES
            if g == 0:
                w_bf[i] = pair_pool.tile([P, 2, H * PACK], BF16, name="w_bf_pair", align_bytes=64)
            elif g == 1:
                w_bf[i] = w_bf[i - 1]
            else:
                w_bf[i] = bf_pool.tile([P, 1, H * PACK], BF16, name="w_bf", align_bytes=64)
            dst = w_bf[i][:, g % 2].rearrange("p (t m j) -> p m j t", t=PACK, j=PACK)
            src = w_raw[i][:].rearrange("p j (m t) -> p m j t", t=PACK)
            if ENGINE[i] == "L":
                for q in range(2):
                    m0 = 64 * q
                    copy_on("S", dst[:, m0 : m0 + L_CUT], src[:, m0 : m0 + L_CUT])
                    copy_on("V", dst[:, m0 + L_CUT : m0 + 64], src[:, m0 + L_CUT : m0 + 64])
            elif ENGINE[i] == "M":
                copy_on("S", dst[:, :M_CUT], src[:, :M_CUT])
                copy_on("V", dst[:, M_CUT:], src[:, M_CUT:])
            else:
                copy_on(ENGINE[i], dst, src)

        def quantize(i):
            if i % PASSES == 0:
                return
            n = 2 if i % PASSES == 1 else 1
            codes = code_pool.tile([P, n * H], U32, name=f"w_codes{n}", align_bytes=64)
            scales = code_pool.tile([P, n * H], U8, name=f"w_scales{n}", align_bytes=64)
            for k in range(n):
                w_codes[i - n + 1 + k] = codes[:, k * H : (k + 1) * H]
                w_scales[i - n + 1 + k] = scales[:, k * H : (k + 1) * H]
            parts = 2 if i == last else 1
            flat = w_bf[i][:].rearrange("p g n -> p (g n)")
            for q in range(parts):
                cols = slice(q * n * H // parts, (q + 1) * n * H // parts)
                nc.vector.quantize_mx(
                    out=codes[:, cols].bitcast(FP8X4),
                    scales=scales[:, cols],
                    in_=flat[:, q * n * H * PACK // parts : (q + 1) * n * H * PACK // parts],
                )

        def interleave_w2(e, engine):
            dst = w2_bf[:, e * N * PACK : (e + 1) * N * PACK].rearrange("p (c i j) -> p c j i", i=4, j=PACK)
            src = w2_raw[:, e].rearrange("p j (c i) -> p c j i", i=4)
            copy_on(engine, dst, src)

        def quantize_w2(e0, e1):
            cols = slice(e0 * N, e1 * N)
            nc.vector.quantize_mx(
                out=w2_codes[:, cols].bitcast(FP8X4),
                scales=w2_scales[:, cols],
                in_=w2_bf[:, e0 * N * PACK : e1 * N * PACK],
            )

        def layer1_pass(acc, e, g, t, c0, c1):
            i = PASSES * e + g
            s, base = slice_of[e]
            m_cols = slice(t * P, (t + 1) * P)
            n_cols = slice(base + c0, base + c1)
            nc.tensor.matmul_mx(
                out=acc,
                lhsT=w_codes[i][:, m_cols].bitcast(FP8X4),
                lhsT_scale=w_scales[i][:, m_cols],
                rhs=slot_words[s, g][:, n_cols].bitcast(FP8X4),
                rhs_scale=slot_bytes[s][4 * g : P, n_cols],
                start=(g == 0),
                stop=(g == PASSES - 1),
            )

        def layer1(e):
            accs = []
            for half in range(2):
                acc = psum.tile([P, PACK, HALF], F32, name="acc")
                for t in range(PACK):
                    for g in range(PASSES):
                        layer1_pass(acc[:, t, :], e, g, t, half * HALF, (half + 1) * HALF)
                accs.append(acc)
            return accs

        def silu(e, accs):
            h_bf = raw_pool.tile([P, C * PACK], BF16, name=f"h_bf{e}", offset=raw_place(BEHIND[e]), align_bytes=64)
            for half in range(2):
                nc.scalar.activation(
                    h_bf[:, half * HALF * PACK : (half + 1) * HALF * PACK].rearrange("p (n t) -> p n t", t=PACK),
                    accs[half][:].rearrange("p t n -> p n t"),
                    SILU,
                )
            return h_bf

        def quantize_h(h_bf):
            h_codes = h_pool.tile([P, C], U32, name="h_codes", align_bytes=64)
            h_scales = h_pool.tile([P, C], U8, name="h_scales", align_bytes=64)
            nc.vector.quantize_mx(out=h_codes[:].bitcast(FP8X4), scales=h_scales[:], in_=h_bf[:])
            return h_codes, h_scales

        def layer2(y, e, h, c0, c1):
            h_codes, h_scales = h
            m_cols = slice(e * N, (e + 1) * N)
            nc.tensor.matmul_mx(
                out=y,
                lhsT=w2_codes[:, m_cols].bitcast(FP8X4),
                lhsT_scale=w2_scales[:, m_cols],
                rhs=h_codes[:, c0:c1].bitcast(FP8X4),
                rhs_scale=h_scales[:, c0:c1],
                start=True,
                stop=True,
            )

        gather(0)
        gather(1)
        def prepare_w2(pair):
            for d in (2 * pair, 2 * pair + 1):
                interleave_w2(d, W2E[d])
            quantize_w2(2 * pair, 2 * pair + 2)

        def results(pair):
            e0 = 2 * pair
            if pair < 2:
                y = y_psum.tile([P, 2, C], F32, name="y_pair")
                for d in (e0, e0 + 1):
                    layer2(y[:, d - e0], d, h_of[d], 0, C)
                copy_on(YE[pair], y_all[:, e0 * C : (e0 + 2) * C], y[:].rearrange("p e n -> p (e n)"))
            else:
                y = psum.tile([P, C], F32, name="acc")
                layer2(y[:], 4, h_of[4], 0, C)
                copy_on(YE[2], y_all[:, 4 * C : 5 * C], y[:])

        acc_of = {}

        h_of = {}

        def finish(e):
            h_of[e] = quantize_h(silu(e, acc_of[e]))

        last_acc = []
        for i, (e, g) in enumerate(chunks):
            interleave(i)
            for pair, at in enumerate(W2_AT):
                if i == at + 1:
                    prepare_w2(pair)
            for b, behind in enumerate(BEHIND):
                if i == behind:
                    finish(b)
            for pair, at in enumerate(W2_AT):
                if i == max(at + 1, BEHIND[min(2 * pair + 1, 4)]):
                    results(pair)
            if i + RAW <= last:
                load(i + RAW)
            quantize(i)
            if e < E - 1 and g == PASSES - 1:
                acc_of[e] = layer1(e)
            for k, at in enumerate(GATHER_AT):
                if i == at:
                    gather(2 + k)
            if e == E - 1:
                if g == 0:
                    last_acc = [psum.tile([P, C], F32, name="acc") for t in range(PACK)]
                for gg in ((), (0, 1), (2,))[g]:
                    for t in range(PACK):
                        layer1_pass(last_acc[t][:], e, gg, t, 0, C)

        h_rows = end_pool.tile([P, PACK, C], BF16, name="h_rows")
        for t in range(PACK):
            nc.scalar.activation(h_rows[:, t, :], last_acc[t][:], SILU)
        for pair in range(3):
            if W2_AT[pair] == last:
                prepare_w2(pair)
                results(pair)
        h_last = end_pool.tile([P, C * PACK], BF16, name="h_last", align_bytes=64)
        nc.vector.tensor_copy(
            out=h_last[:].rearrange("p (c i t) -> p c t i", i=4, t=PACK),
            in_=h_rows[:].rearrange("p t (c i) -> p c t i", i=4),
        )
        h = quantize_h(h_last)
        y = psum.tile([P, C], F32, name="acc")
        layer2(y[:], E - 1, h, 0, C)
        nc.vector.tensor_copy(out=y_all[:, (E - 1) * C :], in_=y[:])

        for back in range(len(BACK)):
            t0 = sum(BACK[:back])
            t1 = t0 + BACK[back]
            cols = slice(t0, t1)
            part = [end_pool.tile([P, t1 - t0], F32, name=f"part{r}_{t0}") for r in range(2)]
            for r in range(2):
                nc.vector.tensor_tensor(
                    part[r][:],
                    y_all[:].indirect(pos_t[r][:, t0 // 16 : t1 // 16]),
                    gate_t[:, r, cols],
                    MULT,
                )
            total = end_pool.tile([P, t1 - t0], F32, name=f"total_{t0}")
            nc.vector.tensor_tensor(total[:], part[0][:], part[1][:], ADD)
            nc.sync.dma_start(out=out[:, cols], in_=total[:])
